import numpy as np
import ml_dtypes


def mxq(x, axis, fmt="e4m3"):
    dtype, down = {"e4m3": (ml_dtypes.float8_e4m3fn, 7), "e5m2": (ml_dtypes.float8_e5m2, 14)}[fmt]
    v = np.moveaxis(np.asarray(x, np.float32).astype(ml_dtypes.bfloat16).astype(np.float64), axis, -1)
    blocks = v.reshape(v.shape[:-1] + (-1, 32))
    amax = np.abs(blocks).max(-1, keepdims=True)
    byte = np.maximum(np.where(amax > 0, np.frexp(amax)[1] - 1 + 127, 0) - down, 1)
    scale = np.exp2(byte - 127.0)
    codes = (blocks / scale).astype(np.float32).astype(dtype).astype(np.float64)
    return np.moveaxis((codes * scale).reshape(v.shape), -1, axis)


WIDE = False


def mx_kscale(k):
    if not WIDE:
        return np.ones(k)
    levels = np.array([10, -10, 5, -5, 0])
    if k % 512:
        return np.exp2(np.random.permutation(np.resize(levels, k // 32))).repeat(32)
    a = np.empty((k // 512, 16))
    for p in range(k // 512):
        a[p, :8] = np.random.permutation(np.resize(levels, 8))
        for g in range(8):
            far = levels[np.abs(levels - a[p, g]) >= 10]
            a[p, g + 8] = far[np.random.randint(len(far))]
    return np.exp2(a.ravel()).repeat(32)


def f64(x):
    return np.asarray(x).astype(np.float64)


def striped(idx):
    return np.tile(idx.reshape(-1, 16).T, (8, 1)).astype(np.uint16)


def unstriped(offs):
    return offs[:16].T.reshape(-1).astype(np.int64)


def striped8(idx):
    return np.concatenate([x.reshape(-1, 16).T for x in idx]).astype(np.uint16)


def runs(offs, k):
    lists = np.stack([offs[16 * r : 16 * r + 16].T.reshape(-1) for r in range(8)]).astype(np.int64)
    return lists[np.arange(k) % 512 // 64]


def pack_weight(w):
    k, n = w.shape
    w = f64(np.asarray(w, np.float32).astype(ml_dtypes.bfloat16)).reshape(k // 32, 32, n)
    amax = np.abs(w).max(1)
    byte = np.clip(np.where(amax > 0, np.frexp(amax)[1] - 1 + 127 - 7, 1), 1, 254)
    scaled = (w * np.exp2(127.0 - byte)[:, None, :]).reshape(k, n).astype(np.float32)
    words = np.ascontiguousarray(scaled.reshape(k // 512, 128, 4, n).transpose(0, 1, 3, 2)).astype(ml_dtypes.float8_e4m3fn).view(np.uint8)
    return words, np.ascontiguousarray(byte.astype(np.uint8).reshape(k // 512, 16, n))


def unpack_weight(words, scales):
    g, p, n, _ = words.shape
    vals = np.ascontiguousarray(words).view(ml_dtypes.float8_e4m3fn).astype(np.float64) * np.repeat(np.exp2(scales.astype(np.float64) - 127.0), 8, axis=1)[..., None]
    return vals.transpose(0, 1, 3, 2).reshape(g * 512, n)


def relu(v):
    return np.maximum(v, 0.0)


K, T, S, N, G, H = 512, 2048, 512, 512, 2048, 512


def setup_inputs():
    n = np.random.standard_normal
    s = mx_kscale(K)[:, None]
    u = mx_kscale(H)
    packed_xT = pack_weight(n((K, T)) * s)
    packed_dT = pack_weight(n((K, G)) / s)
    return {
        "x_words": packed_xT[0],
        "x_scales": packed_xT[1],
        "d_words": packed_dT[0],
        "d_scales": packed_dT[1],
        "gn": (np.random.uniform(0.5, 1.5, (H, 1)) * u[:, None]).astype(np.float32),
        "w1": (n((H, N)) / np.sqrt(H) / u[:, None]).astype(np.float32),
        "offs": striped(np.random.permutation(T)[:S]),
        "kidx": striped8(np.random.randint(0, G, (8, H))),
        "n1": striped8(np.stack([np.random.permutation(S) for _ in range(8)])),
        "n2": striped8(np.stack([np.random.permutation(S) for _ in range(8)])),
    }


def reference(x_words, x_scales, d_words, d_scales, gn, w1, offs, kidx, n1, n2):
    d_kidx = unpack_weight(d_words, d_scales)[np.arange(K)[:, None], runs(kidx, K)]
    xq = unpack_weight(x_words, x_scales)[:, unstriped(offs)]
    s = 0.0625 * (d_kidx.T @ xq)
    z = f64(gn) * (relu(s - (0.5 * (np.maximum(s[np.arange(H)[:, None], runs(n1, H)], s[np.arange(H)[:, None], runs(n2, H)])))))
    return mxq(f64(w1), 0, "e4m3").T @ mxq(z, 0, "e4m3")

@@ -1,0 +1,178 @@
+from contextlib import ExitStack
+
+import concourse.mybir as mybir
+
+F32 = mybir.dt.float32
+BF16 = mybir.dt.bfloat16
+I32 = mybir.dt.int32
+U32 = mybir.dt.uint32
+U16 = mybir.dt.uint16
+U8 = mybir.dt.uint8
+FP8X4 = mybir.dt.float8_e4m3fn_x4
+ALU = mybir.AluOpType
+ACT = mybir.ActivationFunctionType
+
+P = 128
+PACK = 4
+K, T, S, N, G, H = 512, 2048, 512, 512, 2048, 512
+FLOPS = 2 * K * H * S + 2 * H * N * S
+CHUNKS = ((0, 256), (256, 128), (384, 128))
+
+
+def tile_picked_scoreinh_none_p_kernel(
+    tc, x_words, x_scales, d_words, d_scales, gn, w1, offs, kidx, n1, n2, out
+):
+    nc = tc.nc
+    with ExitStack() as ctx:
+        keep = ctx.enter_context(tc.tile_pool(name="keep", bufs=1))
+        psum = ctx.enter_context(tc.psum_pool(name="psum", bufs=1))
+
+        kidx_t = keep.tile([P, H // 16], U16, name="kidx_t")
+        offs_t = keep.tile([P, S // 16], U16, name="offs_t")
+        n1_t = keep.tile([P, S // 16], U16, name="n1_t")
+        n2_t = keep.tile([P, S // 16], U16, name="n2_t")
+        dw_win = keep.tile([P, G], U32, name="dw_win", align_bytes=64)
+        xw_win = keep.tile([P, T], U32, name="xw_win", align_bytes=64)
+        ds_win = keep.tile([P, G], U8, name="ds_win", tag="d_stage", align_bytes=64)
+        xs_win = keep.tile([P, T], U8, name="xs_win", align_bytes=64)
+        d_plane = keep.tile([P, H], U8, name="d_plane", align_bytes=64)
+        gn_t = keep.tile([P, PACK], F32, name="gn_t")
+        w_raw = keep.tile([P, PACK, N], F32, name="w_raw")
+
+        nc.vector.memset(ds_win[:].bitcast(I32), 0)
+        nc.vector.memset(xs_win[:].bitcast(I32), 0)
+        nc.vector.memset(d_plane[:].bitcast(I32), 0)
+
+        nc.sync.dma_start(kidx_t[:], kidx)
+        nc.scalar.dma_start(ds_win[0:P:8, :].bitcast(I32), d_scales[0].bitcast(I32))
+        nc.sync.dma_start(dw_win[:].bitcast(I32), d_words[0].rearrange("p n t -> p (n t)").bitcast(I32))
+        nc.sync.dma_start(offs_t[:], offs)
+        nc.sync.dma_start(n1_t[:], n1)
+        nc.sync.dma_start(xw_win[:].bitcast(I32), x_words[0].rearrange("p n t -> p (n t)").bitcast(I32))
+        nc.sync.dma_start(n2_t[:], n2)
+        nc.sync.dma_start(w_raw[:], w1.rearrange("(p t) m -> p t m", t=PACK))
+        nc.gpsimd.dma_start(gn_t[:], gn.rearrange("(p t) o -> p (t o)", t=PACK))
+        for a in range(4):
+            nc.gpsimd.dma_start(xs_win[a:P:32, :].bitcast(I32), x_scales[0, a:16:4, :].bitcast(I32))
+
+        g_half = keep.tile([P, PACK], F32, name="g_half")
+        g_full = keep.tile([P, PACK], F32, name="g_full")
+        g_nonneg = keep.tile([P, PACK], F32, name="g_nonneg")
+        g_sign = keep.tile([P, PACK], F32, name="g_sign")
+        nc.scalar.activation(g_half[:], gn_t[:], ACT.Abs, scale=0.03125)
+        nc.scalar.activation(g_full[:], gn_t[:], ACT.Abs, scale=0.0625)
+        nc.gpsimd.tensor_scalar(g_nonneg[:], gn_t[:], 0.0, 2.0, ALU.is_ge, ALU.mult)
+        nc.gpsimd.tensor_scalar(g_sign[:], g_nonneg[:], 1.0, -1.0, ALU.mult, ALU.add)
+
+        ds_got = keep.tile([P, H], U8, name="ds_got", align_bytes=64)
+        ds_dealt = keep.tile([P, PACK, P], U8, name="ds_dealt", align_bytes=64)
+        nc.vector.tensor_copy(ds_got[:], ds_win[:].indirect(kidx_t[:]))
+        nc.vector.tensor_copy(ds_dealt[:], ds_got[:].rearrange("p (m t) -> p t m", t=PACK))
+        for a in range(4):
+            nc.scalar.dma_start(
+                d_plane[a:P:32, :].bitcast(I32),
+                ds_dealt[8 * a : P : 32, :, :].rearrange("p t m -> p (t m)").bitcast(I32),
+            )
+
+        dw_got = keep.tile([P, H], U32, name="dw_got", tag="d_stage", align_bytes=64)
+        dw_dealt = keep.tile([P, PACK, P], U32, name="dw_dealt", align_bytes=64)
+        nc.vector.tensor_copy(dw_got[:], dw_win[:].indirect(kidx_t[:]))
+        nc.vector.tensor_copy(
+            dw_dealt[:].bitcast(I32).rearrange("p t (c i) -> p c t i", i=4),
+            dw_got[:].bitcast(I32).rearrange("p (c i t) -> p c t i", i=4, t=PACK),
+        )
+        xs_got = keep.tile([P, S], U8, name="xs_got", align_bytes=64)
+        xw_got = keep.tile([P, S], U32, name="xw_got", align_bytes=64)
+        for h in range(2):
+            nc.vector.tensor_copy(xs_got[:, 256 * h : 256 * (h + 1)], xs_win[:].indirect(offs_t[:, 16 * h : 16 * (h + 1)]))
+            nc.vector.tensor_copy(xw_got[:, 256 * h : 256 * (h + 1)], xw_win[:].indirect(offs_t[:, 16 * h : 16 * (h + 1)]))
+
+        half = [keep.tile([P, S], F32, name="half%d" % t) for t in range(PACK)]
+        full = [keep.tile([P, S], F32, name="full%d" % t) for t in range(PACK)]
+        score = {}
+        for h in range(2):
+            for t in range(PACK):
+                score[t, h] = psum.tile([P, 512], F32, name="bank%d" % (PACK * h + t))
+                nc.tensor.matmul_mx(
+                    out=score[t, h][:, 0:256],
+                    lhsT=dw_dealt[:, t, :].bitcast(FP8X4),
+                    lhsT_scale=d_plane[:, P * t : P * (t + 1)],
+                    rhs=xw_got[:, 256 * h : 256 * (h + 1)].bitcast(FP8X4),
+                    rhs_scale=xs_got[:, 256 * h : 256 * (h + 1)],
+                    start=True,
+                    stop=True,
+                )
+
+        def scaled(dst, factor, t, h):
+            nc.scalar.activation(dst[t][:, 256 * h : 256 * (h + 1)], score[t, h][:, 0:256], ACT.Copy, scale=factor[:, t : t + 1])
+
+        for t in range(PACK):
+            scaled(half, g_half, t, 0)
+            scaled(full, g_full, t, 0)
+            scaled(half, g_half, t, 1)
+        for t in range(PACK):
+            scaled(full, g_full, t, 1)
+        bank_no = 0
+
+        w_signed = keep.tile([P, PACK, N], BF16, name="w_signed")
+        w_woven = keep.tile([P, N, PACK], BF16, name="w_woven", align_bytes=64)
+        w_codes = keep.tile([P, N], U32, name="w_codes", align_bytes=64)
+        w_plane = keep.tile([P, N], U8, name="w_plane", align_bytes=64)
+        for t in range(PACK):
+            nc.scalar.activation(w_signed[:, t, :], w_raw[:, t, :], ACT.Copy, scale=g_sign[:, t : t + 1])
+        for m0 in range(0, N, P):
+            nc.scalar.copy(
+                w_woven[:, m0 : m0 + P, :].rearrange("p (c i) t -> p c t i", i=4),
+                w_signed[:, :, m0 : m0 + P].rearrange("p t (c i) -> p c t i", i=4),
+            )
+
+        out_v = out.rearrange("(mt p) j -> p mt j", p=P)
+        for ci, (c0, w) in enumerate(CHUNKS):
+            last = ci == len(CHUNKS) - 1
+            tags = {1: "z_woven0", 3: "z_woven1"} if last else {}
+            d1 = [keep.tile([P, w], F32, name="d1_%d_%d" % (ci, t), tag=tags.get(t, "d1_%d_%d" % (ci, t)), align_bytes=64) for t in range(PACK)]
+            d2 = keep.tile([P, PACK, w], F32, name="d2_%d" % ci)
+            dmax = keep.tile([P, PACK, w], F32, name="dmax_%d" % ci)
+            cols16 = slice(c0 // 16, (c0 + w) // 16)
+            for t in range(PACK):
+                nc.vector.tensor_tensor(d1[t][:], half[t][:].indirect(n1_t[:, cols16]), full[t][:, c0 : c0 + w], ALU.subtract)
+                nc.vector.tensor_tensor(d2[:, t, :], half[t][:].indirect(n2_t[:, cols16]), full[t][:, c0 : c0 + w], ALU.subtract)
+                if t > 0:
+                    nc.vector.tensor_tensor(dmax[:, t - 1, :], d1[t - 1][:], d2[:, t - 1, :], ALU.max)
+            nc.vector.tensor_tensor(dmax[:, PACK - 1, :], d1[PACK - 1][:], d2[:, PACK - 1, :], ALU.max)
+            z_woven = keep.tile([P, w, PACK], BF16, name="z_woven%d" % ci, tag="z_woven%d" % ci, align_bytes=64)
+            if last:
+                nc.vector.tensor_scalar(z_woven[:], dmax[:].rearrange("p t j -> p j t"), -1.0, 0.0, ALU.mult, ALU.max)
+            else:
+                nc.scalar.activation(z_woven[:], dmax[:].rearrange("p t j -> p j t"), ACT.Relu, scale=-1.0)
+            if ci == 0:
+                nc.vector.quantize_mx(out=w_codes[:].bitcast(FP8X4), scales=w_plane[:], in_=w_woven[:].rearrange("p m t -> p (m t)"))
+            z_codes = keep.tile([P, w], U32, name="z_codes%d" % ci, align_bytes=64)
+            z_plane = keep.tile([P, w], U8, name="z_plane%d" % ci, align_bytes=64)
+            nc.vector.quantize_mx(out=z_codes[:].bitcast(FP8X4), scales=z_plane[:], in_=z_woven[:].rearrange("p j t -> p (j t)"))
+            res = keep.tile([P, N // P, w], F32, name="res%d" % ci)
+            per_bank = 2
+            for b in range(N // P // per_bank):
+                bank = psum.tile([P, 512], F32, name="bank%d" % (bank_no % 8))
+                bank_no = bank_no + 1
+                for i in range(per_bank):
+                    mt = b * per_bank + i
+                    nc.tensor.matmul_mx(
+                        out=bank[:, i * w : (i + 1) * w],
+                        lhsT=w_codes[:, P * mt : P * (mt + 1)].bitcast(FP8X4),
+                        lhsT_scale=w_plane[:, P * mt : P * (mt + 1)],
+                        rhs=z_codes[:].bitcast(FP8X4),
+                        rhs_scale=z_plane[:],
+                        start=True,
+                        stop=True,
+                    )
+                dst = res[:, b * per_bank : (b + 1) * per_bank, :].rearrange("p i j -> p (i j)")
+                if last and b == 1:
+                    nc.vector.tensor_copy(dst, bank[:, 0 : per_bank * w])
+                else:
+                    nc.scalar.copy(dst, bank[:, 0 : per_bank * w])
+                if last:
+                    queue = nc.sync if b == 1 else nc.scalar
+                    queue.dma_start(out_v[:, b * per_bank : (b + 1) * per_bank, c0 : c0 + w], res[:, b * per_bank : (b + 1) * per_bank, :])
+            if not last:
+                nc.sync.dma_start(out_v[:, :, c0 : c0 + w], res[:])

@@ -32,121 +32,155 @@ def tile_picked_scoreinh_none_p_kernel(
         n1_t = keep.tile([P, S // 16], U16, name="n1_t")
         n2_t = keep.tile([P, S // 16], U16, name="n2_t")
         dw_win = keep.tile([P, G], U32, name="dw_win", align_bytes=64)
-        xw_win = keep.tile([P, T], U32, name="xw_win", align_bytes=64)
-        ds_win = keep.tile([P, G], U8, name="ds_win", tag="d_stage", align_bytes=64)
-        xs_win = keep.tile([P, T], U8, name="xs_win", align_bytes=64)
-        d_plane = keep.tile([P, H], U8, name="d_plane", align_bytes=64)
+        xw_win = keep.tile([P, T], U32, name="xw_win", tag="x_then_w", align_bytes=64)
+        ds_win = keep.tile([P, G], U8, name="ds_win", align_bytes=64)
+        xs_win = keep.tile([P, T], U8, name="xs_win", tag="x_stage", align_bytes=64)
+        planes = keep.tile([P, H + S], U8, name="planes", align_bytes=64)
         gn_t = keep.tile([P, PACK], F32, name="gn_t")
-        w_raw = keep.tile([P, PACK, N], F32, name="w_raw")
 
         nc.vector.memset(ds_win[:].bitcast(I32), 0)
-        nc.vector.memset(xs_win[:].bitcast(I32), 0)
-        nc.vector.memset(d_plane[:].bitcast(I32), 0)
+        nc.gpsimd.memset(xs_win[:, 0:1408].bitcast(I32), 0)
+        nc.vector.memset(xs_win[:, 1408:T].bitcast(I32), 0)
 
         nc.sync.dma_start(kidx_t[:], kidx)
-        nc.scalar.dma_start(ds_win[0:P:8, :].bitcast(I32), d_scales[0].bitcast(I32))
-        nc.sync.dma_start(dw_win[:].bitcast(I32), d_words[0].rearrange("p n t -> p (n t)").bitcast(I32))
+        nc.sync.dma_start(ds_win[0:P:8, :].bitcast(I32), d_scales[0].bitcast(I32))
+        nc.sync.dma_start(xs_win[0:P:8, :].bitcast(I32), x_scales[0].bitcast(I32))
         nc.sync.dma_start(offs_t[:], offs)
         nc.sync.dma_start(n1_t[:], n1)
-        nc.sync.dma_start(xw_win[:].bitcast(I32), x_words[0].rearrange("p n t -> p (n t)").bitcast(I32))
         nc.sync.dma_start(n2_t[:], n2)
-        nc.sync.dma_start(w_raw[:], w1.rearrange("(p t) m -> p t m", t=PACK))
         nc.gpsimd.dma_start(gn_t[:], gn.rearrange("(p t) o -> p (t o)", t=PACK))
-        for a in range(4):
-            nc.gpsimd.dma_start(xs_win[a:P:32, :].bitcast(I32), x_scales[0, a:16:4, :].bitcast(I32))
+        nc.gpsimd.memset(planes[:].bitcast(I32), 0)
+        w1_v = w1.rearrange("(p t) m -> p t m", t=PACK)
+        nc.sync.dma_start(dw_win[:].bitcast(I32), d_words[0].rearrange("p n t -> p (n t)").bitcast(I32))
+        nc.sync.dma_start(xw_win[:].bitcast(I32), x_words[0].rearrange("p n t -> p (n t)").bitcast(I32))
 
         g_half = keep.tile([P, PACK], F32, name="g_half")
         g_full = keep.tile([P, PACK], F32, name="g_full")
         g_nonneg = keep.tile([P, PACK], F32, name="g_nonneg")
         g_sign = keep.tile([P, PACK], F32, name="g_sign")
-        nc.scalar.activation(g_half[:], gn_t[:], ACT.Abs, scale=0.03125)
         nc.scalar.activation(g_full[:], gn_t[:], ACT.Abs, scale=0.0625)
+        nc.scalar.activation(g_half[:], g_full[:], ACT.Copy, scale=-0.5)
         nc.gpsimd.tensor_scalar(g_nonneg[:], gn_t[:], 0.0, 2.0, ALU.is_ge, ALU.mult)
         nc.gpsimd.tensor_scalar(g_sign[:], g_nonneg[:], 1.0, -1.0, ALU.mult, ALU.add)
 
-        ds_got = keep.tile([P, H], U8, name="ds_got", align_bytes=64)
-        ds_dealt = keep.tile([P, PACK, P], U8, name="ds_dealt", align_bytes=64)
-        nc.vector.tensor_copy(ds_got[:], ds_win[:].indirect(kidx_t[:]))
-        nc.vector.tensor_copy(ds_dealt[:], ds_got[:].rearrange("p (m t) -> p t m", t=PACK))
+        s_got = keep.tile([P, H + S], U8, name="s_got", align_bytes=64)
+        nc.vector.tensor_copy(s_got[:, 0:H], ds_win[:].indirect(kidx_t[:]))
+        nc.vector.tensor_copy(s_got[:, H : H + S], xs_win[:].indirect(offs_t[:]))
         for a in range(4):
-            nc.scalar.dma_start(
-                d_plane[a:P:32, :].bitcast(I32),
-                ds_dealt[8 * a : P : 32, :, :].rearrange("p t m -> p (t m)").bitcast(I32),
-            )
+            nc.sync.dma_start(planes[a:P:32, :].bitcast(I32), s_got[8 * a : P : 32, :].bitcast(I32))
 
-        dw_got = keep.tile([P, H], U32, name="dw_got", tag="d_stage", align_bytes=64)
+        dw_got = keep.tile([P, H], U32, name="dw_got", tag="x_stage", align_bytes=64)
         dw_dealt = keep.tile([P, PACK, P], U32, name="dw_dealt", align_bytes=64)
         nc.vector.tensor_copy(dw_got[:], dw_win[:].indirect(kidx_t[:]))
-        nc.vector.tensor_copy(
-            dw_dealt[:].bitcast(I32).rearrange("p t (c i) -> p c t i", i=4),
-            dw_got[:].bitcast(I32).rearrange("p (c i t) -> p c t i", i=4, t=PACK),
-        )
-        xs_got = keep.tile([P, S], U8, name="xs_got", align_bytes=64)
+
+        def deal_words(t0, t1):
+            nc.vector.tensor_copy(
+                dw_dealt[:, t0:t1, :].bitcast(I32).rearrange("p t (c i) -> p c t i", i=4),
+                dw_got[:].bitcast(I32).rearrange("p (c i t) -> p c t i", i=4, t=PACK)[:, :, t0:t1, :],
+            )
+
+        d_plane = keep.tile([P, PACK, P], U8, name="d_plane", align_bytes=64)
+
+        def deal_scales(t0, t1):
+            nc.vector.tensor_copy(d_plane[:, t0:t1, :], planes[:, 0:H].rearrange("p (m t) -> p t m", t=PACK)[:, t0:t1, :])
+
+        deal_words(0, 1)
         xw_got = keep.tile([P, S], U32, name="xw_got", align_bytes=64)
         for h in range(2):
-            nc.vector.tensor_copy(xs_got[:, 256 * h : 256 * (h + 1)], xs_win[:].indirect(offs_t[:, 16 * h : 16 * (h + 1)]))
             nc.vector.tensor_copy(xw_got[:, 256 * h : 256 * (h + 1)], xw_win[:].indirect(offs_t[:, 16 * h : 16 * (h + 1)]))
+        deal_scales(0, 1)
+        deal_words(1, PACK)
+        deal_scales(1, PACK)
+        w_raw = keep.tile([P, PACK, N], F32, name="w_raw", tag="x_then_w", align_bytes=64)
+        nc.sync.dma_start(w_raw[:], w1_v)
+
+        w_codes = [keep.tile([P, 256], U32, name="w_codes%d" % h, align_bytes=64) for h in range(2)]
+        w_plane = [keep.tile([P, 256], U8, name="w_plane%d" % h, align_bytes=64) for h in range(2)]
+        w_woven = [keep.tile([P, 256, PACK], BF16, name="w_woven%d" % h, tag="w_woven%d" % h, align_bytes=64) for h in range(2)]
+
+        def weave_w(h):
+            w_signed = keep.tile([P, PACK, 256], BF16, name="w_signed%d" % h)
+            for t in range(PACK):
+                nc.scalar.activation(w_signed[:, t, :], w_raw[:, t, 256 * h : 256 * (h + 1)], ACT.Copy, scale=g_sign[:, t : t + 1])
+            for m0 in range(0, 256, P):
+                nc.scalar.copy(
+                    w_woven[h][:, m0 : m0 + P, :].rearrange("p (c i) t -> p c t i", i=4),
+                    w_signed[:, :, m0 : m0 + P].rearrange("p t (c i) -> p c t i", i=4),
+                )
+
+        def quantize_w(h):
+            nc.vector.quantize_mx(out=w_codes[h][:].bitcast(FP8X4), scales=w_plane[h][:], in_=w_woven[h][:].rearrange("p m t -> p (m t)"))
+
 
         half = [keep.tile([P, S], F32, name="half%d" % t) for t in range(PACK)]
         full = [keep.tile([P, S], F32, name="full%d" % t) for t in range(PACK)]
-        score = {}
-        for h in range(2):
-            for t in range(PACK):
-                score[t, h] = psum.tile([P, 512], F32, name="bank%d" % (PACK * h + t))
+        for t in range(PACK):
+            pieces = ((0, 256), (256, 256)) if t == 0 else ((0, S),)
+            banks = []
+            for c0, w in pieces:
+                bank = psum.tile([P, 512], F32, name="bank%d" % (t + 4 * (c0 // 256)))
+                banks.append(bank)
                 nc.tensor.matmul_mx(
-                    out=score[t, h][:, 0:256],
+                    out=bank[:, 0:w],
                     lhsT=dw_dealt[:, t, :].bitcast(FP8X4),
-                    lhsT_scale=d_plane[:, P * t : P * (t + 1)],
-                    rhs=xw_got[:, 256 * h : 256 * (h + 1)].bitcast(FP8X4),
-                    rhs_scale=xs_got[:, 256 * h : 256 * (h + 1)],
+                    lhsT_scale=d_plane[:, t, :],
+                    rhs=xw_got[:, c0 : c0 + w].bitcast(FP8X4),
+                    rhs_scale=planes[:, H + c0 : H + c0 + w],
                     start=True,
                     stop=True,
                 )
+            if t == 0:
+                nc.scalar.activation(half[0][:, 0:256], banks[0][:, 0:256], ACT.Copy, scale=g_half[:, 0:1])
+                nc.scalar.activation(half[0][:, 256:512], banks[1][:, 0:256], ACT.Copy, scale=g_half[:, 0:1])
+                nc.vector.tensor_scalar(full[0][:, 0:256], banks[0][:, 0:256], g_full[:, 0:1], None, ALU.mult)
+                late = [(0, banks[1], 0)]
+            else:
+                nc.scalar.activation(half[t][:], banks[0][:], ACT.Copy, scale=g_half[:, t : t + 1])
+                nc.scalar.activation(full[t][:, 0:256], banks[0][:, 0:256], ACT.Copy, scale=g_full[:, t : t + 1])
+                late.append((t, banks[0], 256))
+        for t, bank, b0 in late:
+            nc.scalar.activation(full[t][:, 256:512], bank[:, b0 : b0 + 256], ACT.Copy, scale=g_full[:, t : t + 1])
+        bank_no = 5
 
-        def scaled(dst, factor, t, h):
-            nc.scalar.activation(dst[t][:, 256 * h : 256 * (h + 1)], score[t, h][:, 0:256], ACT.Copy, scale=factor[:, t : t + 1])
-
-        for t in range(PACK):
-            scaled(half, g_half, t, 0)
-            scaled(full, g_full, t, 0)
-            scaled(half, g_half, t, 1)
-        for t in range(PACK):
-            scaled(full, g_full, t, 1)
-        bank_no = 0
-
-        w_signed = keep.tile([P, PACK, N], BF16, name="w_signed")
-        w_woven = keep.tile([P, N, PACK], BF16, name="w_woven", align_bytes=64)
-        w_codes = keep.tile([P, N], U32, name="w_codes", align_bytes=64)
-        w_plane = keep.tile([P, N], U8, name="w_plane", align_bytes=64)
-        for t in range(PACK):
-            nc.scalar.activation(w_signed[:, t, :], w_raw[:, t, :], ACT.Copy, scale=g_sign[:, t : t + 1])
-        for m0 in range(0, N, P):
-            nc.scalar.copy(
-                w_woven[:, m0 : m0 + P, :].rearrange("p (c i) t -> p c t i", i=4),
-                w_signed[:, :, m0 : m0 + P].rearrange("p t (c i) -> p c t i", i=4),
-            )
+        weave_w(0)
+        weave_w(1)
 
         out_v = out.rearrange("(mt p) j -> p mt j", p=P)
         for ci, (c0, w) in enumerate(CHUNKS):
             last = ci == len(CHUNKS) - 1
-            tags = {1: "z_woven0", 3: "z_woven1"} if last else {}
-            d1 = [keep.tile([P, w], F32, name="d1_%d_%d" % (ci, t), tag=tags.get(t, "d1_%d_%d" % (ci, t)), align_bytes=64) for t in range(PACK)]
-            d2 = keep.tile([P, PACK, w], F32, name="d2_%d" % ci)
-            dmax = keep.tile([P, PACK, w], F32, name="dmax_%d" % ci)
+            d1 = keep.tile([P, PACK, w], F32, name="d1_%d" % ci, tag="z_woven0" if last else "d1_%d" % ci, align_bytes=64)
             cols16 = slice(c0 // 16, (c0 + w) // 16)
-            for t in range(PACK):
-                nc.vector.tensor_tensor(d1[t][:], half[t][:].indirect(n1_t[:, cols16]), full[t][:, c0 : c0 + w], ALU.subtract)
-                nc.vector.tensor_tensor(d2[:, t, :], half[t][:].indirect(n2_t[:, cols16]), full[t][:, c0 : c0 + w], ALU.subtract)
-                if t > 0:
-                    nc.vector.tensor_tensor(dmax[:, t - 1, :], d1[t - 1][:], d2[:, t - 1, :], ALU.max)
-            nc.vector.tensor_tensor(dmax[:, PACK - 1, :], d1[PACK - 1][:], d2[:, PACK - 1, :], ALU.max)
             z_woven = keep.tile([P, w, PACK], BF16, name="z_woven%d" % ci, tag="z_woven%d" % ci, align_bytes=64)
             if last:
-                nc.vector.tensor_scalar(z_woven[:], dmax[:].rearrange("p t j -> p j t"), -1.0, 0.0, ALU.mult, ALU.max)
+                d2 = keep.tile([P, 2, w], F32, name="d2_last", tag="w_woven1", align_bytes=64)
+                d2_end = keep.tile([P, 2, w], F32, name="d2_end", tag="z_woven1", align_bytes=64)
+                dmin = keep.tile([P, 2, w], F32, name="dmin")
+                r1 = keep.tile([P, 2, w], F32, name="r1")
+                for t in range(PACK):
+                    nc.vector.tensor_tensor(d1[:, t, :], half[t][:].indirect(n1_t[:, cols16]), full[t][:, c0 : c0 + w], ALU.add)
+                nc.scalar.activation(r1[:], d1[:, 2:4, :], ACT.Relu)
+                for t in range(2):
+                    nc.vector.tensor_tensor(d2[:, t, :], half[t][:].indirect(n2_t[:, cols16]), full[t][:, c0 : c0 + w], ALU.add)
+                nc.vector.tensor_tensor(dmin[:], d1[:, 0:2, :], d2[:], ALU.min)
+                nc.scalar.activation(z_woven[:, :, 0:2], dmin[:].rearrange("p t j -> p j t"), ACT.Relu)
+                for t in range(2, PACK):
+                    nc.vector.tensor_tensor(d2_end[:, t - 2, :], half[t][:].indirect(n2_t[:, cols16]), full[t][:, c0 : c0 + w], ALU.add)
+                nc.vector.scalar_tensor_tensor(
+                    z_woven[:, :, 2:4], d2_end[:].rearrange("p t j -> p j t"), 0.0, r1[:].rearrange("p t j -> p j t"), ALU.max, ALU.min
+                )
             else:
-                nc.scalar.activation(z_woven[:], dmax[:].rearrange("p t j -> p j t"), ACT.Relu, scale=-1.0)
+                d2 = keep.tile([P, PACK, w], F32, name="d2w_%d" % ci)
+                order = [(0, t) for t in range(PACK)] + [(1, t) for t in range(PACK)]
+                if ci == 0:
+                    order = [(k, t) for t in range(PACK) for k in range(2)]
+                for k, t in order:
+                    nc.vector.tensor_tensor((d1, d2)[k][:, t, :], half[t][:].indirect((n1_t, n2_t)[k][:, cols16]), full[t][:, c0 : c0 + w], ALU.add)
+                dmin = keep.tile([P, PACK, w], F32, name="dmin_%d" % ci)
+                nc.vector.tensor_tensor(dmin[:], d1[:], d2[:], ALU.min)
+                nc.scalar.activation(z_woven[:], dmin[:].rearrange("p t j -> p j t"), ACT.Relu)
             if ci == 0:
-                nc.vector.quantize_mx(out=w_codes[:].bitcast(FP8X4), scales=w_plane[:], in_=w_woven[:].rearrange("p m t -> p (m t)"))
+                quantize_w(0)
+                quantize_w(1)
             z_codes = keep.tile([P, w], U32, name="z_codes%d" % ci, align_bytes=64)
             z_plane = keep.tile([P, w], U8, name="z_plane%d" % ci, align_bytes=64)
             nc.vector.quantize_mx(out=z_codes[:].bitcast(FP8X4), scales=z_plane[:], in_=z_woven[:].rearrange("p j t -> p (j t)"))
@@ -156,11 +190,10 @@ def tile_picked_scoreinh_none_p_kernel(
                 bank = psum.tile([P, 512], F32, name="bank%d" % (bank_no % 8))
                 bank_no = bank_no + 1
                 for i in range(per_bank):
-                    mt = b * per_bank + i
                     nc.tensor.matmul_mx(
                         out=bank[:, i * w : (i + 1) * w],
-                        lhsT=w_codes[:, P * mt : P * (mt + 1)].bitcast(FP8X4),
-                        lhsT_scale=w_plane[:, P * mt : P * (mt + 1)],
+                        lhsT=w_codes[b][:, P * i : P * (i + 1)].bitcast(FP8X4),
+                        lhsT_scale=w_plane[b][:, P * i : P * (i + 1)],
                         rhs=z_codes[:].bitcast(FP8X4),
                         rhs_scale=z_plane[:],
                         start=True,

from contextlib import ExitStack

import concourse.mybir as mybir

F32 = mybir.dt.float32
BF16 = mybir.dt.bfloat16
I32 = mybir.dt.int32
U32 = mybir.dt.uint32
U16 = mybir.dt.uint16
U8 = mybir.dt.uint8
FP8X4 = mybir.dt.float8_e4m3fn_x4
ALU = mybir.AluOpType
ACT = mybir.ActivationFunctionType

P = 128
PACK = 4
K, T, S, N, G, H = 512, 2048, 512, 512, 2048, 512
FLOPS = 2 * K * H * S + 2 * H * N * S
CHUNKS = ((0, 256), (256, 128), (384, 128))


def tile_picked_scoreinh_none_p_kernel(
    tc, x_words, x_scales, d_words, d_scales, gn, w1, offs, kidx, n1, n2, out
):
    nc = tc.nc
    with ExitStack() as ctx:
        keep = ctx.enter_context(tc.tile_pool(name="keep", bufs=1))
        psum = ctx.enter_context(tc.psum_pool(name="psum", bufs=1))

        kidx_t = keep.tile([P, H // 16], U16, name="kidx_t")
        offs_t = keep.tile([P, S // 16], U16, name="offs_t")
        n1_t = keep.tile([P, S // 16], U16, name="n1_t")
        n2_t = keep.tile([P, S // 16], U16, name="n2_t")
        dw_win = keep.tile([P, G], U32, name="dw_win", align_bytes=64)
        xw_win = keep.tile([P, T], U32, name="xw_win", tag="x_then_w", align_bytes=64)
        ds_win = keep.tile([P, G], U8, name="ds_win", align_bytes=64)
        xs_win = keep.tile([P, T], U8, name="xs_win", tag="x_stage", align_bytes=64)
        planes = keep.tile([P, H + S], U8, name="planes", align_bytes=64)
        gn_t = keep.tile([P, PACK], F32, name="gn_t")

        nc.vector.memset(ds_win[:].bitcast(I32), 0)
        nc.gpsimd.memset(xs_win[:, 0:1408].bitcast(I32), 0)
        nc.vector.memset(xs_win[:, 1408:T].bitcast(I32), 0)

        nc.sync.dma_start(kidx_t[:], kidx)
        nc.sync.dma_start(ds_win[0:P:8, :].bitcast(I32), d_scales[0].bitcast(I32))
        nc.sync.dma_start(xs_win[0:P:8, :].bitcast(I32), x_scales[0].bitcast(I32))
        nc.sync.dma_start(offs_t[:], offs)
        nc.sync.dma_start(n1_t[:], n1)
        nc.sync.dma_start(n2_t[:], n2)
        nc.gpsimd.dma_start(gn_t[:], gn.rearrange("(p t) o -> p (t o)", t=PACK))
        nc.gpsimd.memset(planes[:].bitcast(I32), 0)
        w1_v = w1.rearrange("(p t) m -> p t m", t=PACK)
        nc.sync.dma_start(dw_win[:].bitcast(I32), d_words[0].rearrange("p n t -> p (n t)").bitcast(I32))
        nc.sync.dma_start(xw_win[:].bitcast(I32), x_words[0].rearrange("p n t -> p (n t)").bitcast(I32))

        g_half = keep.tile([P, PACK], F32, name="g_half")
        g_full = keep.tile([P, PACK], F32, name="g_full")
        g_nonneg = keep.tile([P, PACK], F32, name="g_nonneg")
        g_sign = keep.tile([P, PACK], F32, name="g_sign")
        nc.scalar.activation(g_full[:], gn_t[:], ACT.Abs, scale=0.0625)
        nc.scalar.activation(g_half[:], g_full[:], ACT.Copy, scale=-0.5)
        nc.gpsimd.tensor_scalar(g_nonneg[:], gn_t[:], 0.0, 2.0, ALU.is_ge, ALU.mult)
        nc.gpsimd.tensor_scalar(g_sign[:], g_nonneg[:], 1.0, -1.0, ALU.mult, ALU.add)

        s_got = keep.tile([P, H + S], U8, name="s_got", align_bytes=64)
        nc.vector.tensor_copy(s_got[:, 0:H], ds_win[:].indirect(kidx_t[:]))
        nc.vector.tensor_copy(s_got[:, H : H + S], xs_win[:].indirect(offs_t[:]))
        for a in range(4):
            nc.sync.dma_start(planes[a:P:32, :].bitcast(I32), s_got[8 * a : P : 32, :].bitcast(I32))

        dw_got = keep.tile([P, H], U32, name="dw_got", tag="x_stage", align_bytes=64)
        dw_dealt = keep.tile([P, PACK, P], U32, name="dw_dealt", align_bytes=64)
        nc.vector.tensor_copy(dw_got[:], dw_win[:].indirect(kidx_t[:]))

        def deal_words(t0, t1):
            nc.vector.tensor_copy(
                dw_dealt[:, t0:t1, :].bitcast(I32).rearrange("p t (c i) -> p c t i", i=4),
                dw_got[:].bitcast(I32).rearrange("p (c i t) -> p c t i", i=4, t=PACK)[:, :, t0:t1, :],
            )

        d_plane = keep.tile([P, PACK, P], U8, name="d_plane", align_bytes=64)

        def deal_scales(t0, t1):
            nc.vector.tensor_copy(d_plane[:, t0:t1, :], planes[:, 0:H].rearrange("p (m t) -> p t m", t=PACK)[:, t0:t1, :])

        deal_words(0, 1)
        xw_got = keep.tile([P, S], U32, name="xw_got", align_bytes=64)
        for h in range(2):
            nc.vector.tensor_copy(xw_got[:, 256 * h : 256 * (h + 1)], xw_win[:].indirect(offs_t[:, 16 * h : 16 * (h + 1)]))
        deal_scales(0, 1)
        deal_words(1, PACK)
        deal_scales(1, PACK)
        w_raw = keep.tile([P, PACK, N], F32, name="w_raw", tag="x_then_w", align_bytes=64)
        nc.sync.dma_start(w_raw[:], w1_v)

        w_codes = [keep.tile([P, 256], U32, name="w_codes%d" % h, align_bytes=64) for h in range(2)]
        w_plane = [keep.tile([P, 256], U8, name="w_plane%d" % h, align_bytes=64) for h in range(2)]
        w_woven = [keep.tile([P, 256, PACK], BF16, name="w_woven%d" % h, tag="w_woven%d" % h, align_bytes=64) for h in range(2)]

        def weave_w(h):
            w_signed = keep.tile([P, PACK, 256], BF16, name="w_signed%d" % h)
            for t in range(PACK):
                nc.scalar.activation(w_signed[:, t, :], w_raw[:, t, 256 * h : 256 * (h + 1)], ACT.Copy, scale=g_sign[:, t : t + 1])
            for m0 in range(0, 256, P):
                nc.scalar.copy(
                    w_woven[h][:, m0 : m0 + P, :].rearrange("p (c i) t -> p c t i", i=4),
                    w_signed[:, :, m0 : m0 + P].rearrange("p t (c i) -> p c t i", i=4),
                )

        def quantize_w(h):
            nc.vector.quantize_mx(out=w_codes[h][:].bitcast(FP8X4), scales=w_plane[h][:], in_=w_woven[h][:].rearrange("p m t -> p (m t)"))


        half = [keep.tile([P, S], F32, name="half%d" % t) for t in range(PACK)]
        full = [keep.tile([P, S], F32, name="full%d" % t) for t in range(PACK)]
        for t in range(PACK):
            pieces = ((0, 256), (256, 256)) if t == 0 else ((0, S),)
            banks = []
            for c0, w in pieces:
                bank = psum.tile([P, 512], F32, name="bank%d" % (t + 4 * (c0 // 256)))
                banks.append(bank)
                nc.tensor.matmul_mx(
                    out=bank[:, 0:w],
                    lhsT=dw_dealt[:, t, :].bitcast(FP8X4),
                    lhsT_scale=d_plane[:, t, :],
                    rhs=xw_got[:, c0 : c0 + w].bitcast(FP8X4),
                    rhs_scale=planes[:, H + c0 : H + c0 + w],
                    start=True,
                    stop=True,
                )
            if t == 0:
                nc.scalar.activation(half[0][:, 0:256], banks[0][:, 0:256], ACT.Copy, scale=g_half[:, 0:1])
                nc.scalar.activation(half[0][:, 256:512], banks[1][:, 0:256], ACT.Copy, scale=g_half[:, 0:1])
                nc.vector.tensor_scalar(full[0][:, 0:256], banks[0][:, 0:256], g_full[:, 0:1], None, ALU.mult)
                late = [(0, banks[1], 0)]
            else:
                nc.scalar.activation(half[t][:], banks[0][:], ACT.Copy, scale=g_half[:, t : t + 1])
                nc.scalar.activation(full[t][:, 0:256], banks[0][:, 0:256], ACT.Copy, scale=g_full[:, t : t + 1])
                late.append((t, banks[0], 256))
        for t, bank, b0 in late:
            nc.scalar.activation(full[t][:, 256:512], bank[:, b0 : b0 + 256], ACT.Copy, scale=g_full[:, t : t + 1])
        bank_no = 5

        weave_w(0)
        weave_w(1)

        out_v = out.rearrange("(mt p) j -> p mt j", p=P)
        for ci, (c0, w) in enumerate(CHUNKS):
            last = ci == len(CHUNKS) - 1
            d1 = keep.tile([P, PACK, w], F32, name="d1_%d" % ci, tag="z_woven0" if last else "d1_%d" % ci, align_bytes=64)
            cols16 = slice(c0 // 16, (c0 + w) // 16)
            z_woven = keep.tile([P, w, PACK], BF16, name="z_woven%d" % ci, tag="z_woven%d" % ci, align_bytes=64)
            if last:
                d2 = keep.tile([P, 2, w], F32, name="d2_last", tag="w_woven1", align_bytes=64)
                d2_end = keep.tile([P, 2, w], F32, name="d2_end", tag="z_woven1", align_bytes=64)
                dmin = keep.tile([P, 2, w], F32, name="dmin")
                r1 = keep.tile([P, 2, w], F32, name="r1")
                for t in range(PACK):
                    nc.vector.tensor_tensor(d1[:, t, :], half[t][:].indirect(n1_t[:, cols16]), full[t][:, c0 : c0 + w], ALU.add)
                nc.scalar.activation(r1[:], d1[:, 2:4, :], ACT.Relu)
                for t in range(2):
                    nc.vector.tensor_tensor(d2[:, t, :], half[t][:].indirect(n2_t[:, cols16]), full[t][:, c0 : c0 + w], ALU.add)
                nc.vector.tensor_tensor(dmin[:], d1[:, 0:2, :], d2[:], ALU.min)
                nc.scalar.activation(z_woven[:, :, 0:2], dmin[:].rearrange("p t j -> p j t"), ACT.Relu)
                for t in range(2, PACK):
                    nc.vector.tensor_tensor(d2_end[:, t - 2, :], half[t][:].indirect(n2_t[:, cols16]), full[t][:, c0 : c0 + w], ALU.add)
                nc.vector.scalar_tensor_tensor(
                    z_woven[:, :, 2:4], d2_end[:].rearrange("p t j -> p j t"), 0.0, r1[:].rearrange("p t j -> p j t"), ALU.max, ALU.min
                )
            else:
                d2 = keep.tile([P, PACK, w], F32, name="d2w_%d" % ci)
                order = [(0, t) for t in range(PACK)] + [(1, t) for t in range(PACK)]
                if ci == 0:
                    order = [(k, t) for t in range(PACK) for k in range(2)]
                for k, t in order:
                    nc.vector.tensor_tensor((d1, d2)[k][:, t, :], half[t][:].indirect((n1_t, n2_t)[k][:, cols16]), full[t][:, c0 : c0 + w], ALU.add)
                dmin = keep.tile([P, PACK, w], F32, name="dmin_%d" % ci)
                nc.vector.tensor_tensor(dmin[:], d1[:], d2[:], ALU.min)
                nc.scalar.activation(z_woven[:], dmin[:].rearrange("p t j -> p j t"), ACT.Relu)
            if ci == 0:
                quantize_w(0)
                quantize_w(1)
            z_codes = keep.tile([P, w], U32, name="z_codes%d" % ci, align_bytes=64)
            z_plane = keep.tile([P, w], U8, name="z_plane%d" % ci, align_bytes=64)
            nc.vector.quantize_mx(out=z_codes[:].bitcast(FP8X4), scales=z_plane[:], in_=z_woven[:].rearrange("p j t -> p (j t)"))
            res = keep.tile([P, N // P, w], F32, name="res%d" % ci)
            per_bank = 2
            for b in range(N // P // per_bank):
                bank = psum.tile([P, 512], F32, name="bank%d" % (bank_no % 8))
                bank_no = bank_no + 1
                for i in range(per_bank):
                    nc.tensor.matmul_mx(
                        out=bank[:, i * w : (i + 1) * w],
                        lhsT=w_codes[b][:, P * i : P * (i + 1)].bitcast(FP8X4),
                        lhsT_scale=w_plane[b][:, P * i : P * (i + 1)],
                        rhs=z_codes[:].bitcast(FP8X4),
                        rhs_scale=z_plane[:],
                        start=True,
                        stop=True,
                    )
                dst = res[:, b * per_bank : (b + 1) * per_bank, :].rearrange("p i j -> p (i j)")
                if last and b == 1:
                    nc.vector.tensor_copy(dst, bank[:, 0 : per_bank * w])
                else:
                    nc.scalar.copy(dst, bank[:, 0 : per_bank * w])
                if last:
                    queue = nc.sync if b == 1 else nc.scalar
                    queue.dma_start(out_v[:, b * per_bank : (b + 1) * per_bank, c0 : c0 + w], res[:, b * per_bank : (b + 1) * per_bank, :])
            if not last:
                nc.sync.dma_start(out_v[:, :, c0 : c0 + w], res[:])
